import numpy as np, ml_dtypes
CORES = [1,3,5,9,11,13]
N = 6
R, T, B = 16384, 4096, 256
def entries(a): return a.T.reshape(-1)
def pack(v, P): return np.ascontiguousarray(np.asarray(v, np.int32).reshape(-1, P).T)
def lists(rng, how):
    I = rng.integers(0, N * R, (N, T)); E = np.sort(rng.integers(0, T + 1, (N, B)), axis=1)
    if how == "void":
        E = np.zeros((N, B), np.int64)
        for r in range(N): k = np.sort(1 + rng.permutation(B - 2)[:6]); c = np.sort(1 + rng.permutation(T)[:6]); E[r] = np.concatenate([[0], c])[np.searchsorted(k, np.arange(B), side="right")]
        E[rng.integers(N)] = 0
    if how == "one":
        p = rng.permutation(N); z = rng.integers(0, B, N); z[p[0]] = 0; z[p[1]] = B - 1; E = np.where(np.arange(B)[None, :] < z[:, None], 0, T)
        I[p[::2]] = R * p[1] + I[p[::2]] % R
    if how == "single": E = np.broadcast_to(1 + np.arange(B), (N, B)).copy()
    if how == "hotrank": I = R * int(rng.integers(N)) + rng.integers(0, R, (N, T))
    if how == "edge": I = R * rng.integers(0, N, (N, T)) + np.where(rng.random((N, T)) < 0.5, 0, R - 1); E[:, -1] = T
    return {"idx": np.stack([pack(i, 16) for i in I]), "end": np.stack([pack(v, 16) for v in E])}
def setup_inputs(rng):
    return dict({"tab": rng.standard_normal((N, 128, R), dtype=np.float32).astype(ml_dtypes.bfloat16)}, **lists(rng, "uniform"))
def setup_inputs_edge(rng):
    d = setup_inputs(rng); d.update(lists(rng, "edge"))
    for k in ("tab",): d[k] = (d[k].astype(np.float32) * 1048576.0).astype(d[k].dtype)
    return d
def setup_inputs_hotrank(rng):
    d = setup_inputs(rng); d.update(lists(rng, "hotrank"))
    for k in ("tab",): d[k] = (d[k].astype(np.float32) * (1 / 1024.0)).astype(d[k].dtype)
    return d
def setup_inputs_one(rng):
    d = setup_inputs(rng); d.update(lists(rng, "one"))
    return d
def setup_inputs_single(rng):
    d = setup_inputs(rng); d.update(lists(rng, "single"))
    return d
def setup_inputs_void(rng):
    d = setup_inputs(rng); d.update(lists(rng, "void"))
    return d
def check_inputs(x):
    bad = []
    if x["idx"].min() < 0 or x["idx"].max() >= N * R: bad.append("idx out of range")
    if x["end"].min() < 0 or x["end"].max() >= T + 1: bad.append("end out of range")
    if any((np.diff(entries(a)) < 0).any() for a in x["end"]): bad.append("end falls")
    t = x["tab"].astype(np.float32)
    if t.min() < -1e30 or t.max() > 1e30: bad.append("tab beyond -1e30 to 1e30")
    return bad
def reference(tab, idx, end):
    A = np.concatenate(list(tab), axis=1)
    y = np.zeros((N, 128, B), tab.dtype)
    for r in range(N):
        G = A[:, entries(idx[r])]; c = np.concatenate([[0], entries(end[r])])
        for b in range(B):
            if c[b + 1] > c[b]: y[r][:, b] = G[:, c[b]:c[b + 1]].max(axis=1)
    return {"y": y}

@@ -1,0 +1,357 @@
+from concourse.bass import DstId, RemoteDMATransfer
+from concourse.mybir import AluOpType, ActivationFunctionType
+
+SIM = 16
+R = 16384
+L = 4096
+B = 256
+PAD = 8
+W = R + 2 * PAD
+ZC = L
+SW = L + 8
+MW = L + B
+BIG = 0.999999e30
+CUT = 10240
+NP = 6
+PS = 4
+
+SCRATCH = {
+    "tw": ("sbuf", [128, W], "bfloat16"),
+    "gb": ("sbuf", [128, NP * L], "bfloat16"),
+    "mk": ("sbuf", [128, PS * MW], "bfloat16"),
+    "sc": ("sbuf", [128, PS * SW], "bfloat16"),
+    "neg": ("sbuf", [128, B], "bfloat16"),
+    "pt": ("sbuf", [128, PS * B], "bfloat16"),
+    "ld": ("sbuf", [128, 3 * B], "bfloat16"),
+    "cm": ("sbuf", [128, 3 * B], "bfloat16"),
+    "rp": ("sbuf", [128, 9 * B], "bfloat16"),
+    "ix": ("sbuf", [128, 32], "int32"),
+    "x4": ("sbuf", [128, 4], "int32"),
+    "z1": ("sbuf", [128, 2], "int32"),
+    "z2": ("sbuf", [128, 2], "int32"),
+    "lf": ("sbuf", [128, NP * 32], "float32"),
+    "en": ("sbuf", [128, NP * 32], "uint16"),
+    "of": ("sbuf", [128, NP * 256], "uint16"),
+    "sb4": ("sbuf", [128, 4], "float32"),
+    "bs4": ("sbuf", [128, 4], "float32"),
+    "u4": ("sbuf", [128, 4], "float32"),
+    "ne4": ("sbuf", [128, 4], "float32"),
+    "m4": ("sbuf", [128, 4], "float32"),
+    "r4": ("sbuf", [128, 4], "float32"),
+    "one": ("sbuf", [128, 1024], "float32"),
+    "qq": ("sbuf", [128, 1024], "float32"),
+    "ps0": ("psum", [128, 512], "float32"), "ps1": ("psum", [128, 512], "float32"), "ps2": ("psum", [128, 512], "float32"),
+    "ps3": ("psum", [128, 512], "float32"), "ps4": ("psum", [128, 512], "float32"), "ps5": ("psum", [128, 512], "float32"),
+    "pse": ("psum", [128, 512], "float32"),
+}
+SEMAPHORES = (["dix", "den", "dta", "dtb", "dy", "pace", "ls", "pr0", "pr1", "pr2"]
+              + ["mi%d" % k for k in range(NP)] + ["me%d" % k for k in range(NP)] + ["rp%d" % k for k in range(NP)]
+              + ["st%d" % k for k in range(PS)] + ["v%d" % k for k in range(60)] + ["s%d" % k for k in range(16)]
+              + ["t%d" % k for k in range(8)] + ["q%d" % k for k in range(6)])
+
+
+def layout(T, topo):
+    ranks = list(T.cores)
+    chips = sorted({topo.chip(c) for c in ranks})
+    near, relays, partner = {}, {}, {}
+    for ch in chips:
+        here = [c for c in range(SIM) if topo.chip(c) == ch]
+        away = [c for c in range(SIM) if topo.chip(c) in chips and topo.chip(c) != ch]
+        near[ch] = [c for c in here if c in ranks]
+        spare = [c for c in here if c not in ranks]
+        port = {c: all(topo.may_write(c, d) for d in away) for c in spare}
+        for o in near[ch]:
+            free = [c for c in spare if c not in partner.values()]
+            partner[o] = min(free, key=lambda c: (topo.die(c) != topo.die(o), port[c], c))
+        relays[ch] = [c for c in spare if port[c] and c not in partner.values()]
+    return chips, near, relays, partner
+
+
+def positions(o, topo, chips, near):
+    ch = topo.chip(o)
+    mine = near[ch]
+    j, n = mine.index(o), len(mine)
+    far = [c for k in chips if k != ch for c in near[k]]
+    return [mine[(j + 1) % n]] + far + [mine[(j + 2) % n], o]
+
+
+def engines(topo, src, dsts, n):
+    m = None
+    for d in dsts:
+        m = topo.mask(src, d) if m is None else m & topo.mask(src, d)
+    out, k = 0, 0
+    for b in range(m.bit_length()):
+        if (m >> b) & 1 and k < n:
+            out, k = out | (1 << b), k + 1
+    return out, k
+
+
+def rank_program(g, core, T, topo):
+    chips, near, relays, partner = layout(T, topo)
+    ch = topo.chip(core)
+    if ch not in chips:
+        return
+    mine = near[ch]
+    far = [c for k in chips if k != ch for c in near[k]]
+    far_chip = [k for k in chips if k != ch][0]
+    rk = {c: T.rank_of(c) for c in mine + far}
+
+    def relay_of(chip_, c):
+        rel = relays[chip_]
+        return rel[near[topo.chip(c)].index(c) % len(rel)]
+
+    made, seen, nl = {}, set(), [0]
+    count = {"v": [0], "s": [0], "t": [0], "q": [0]}
+
+    def ev(inst, kind):
+        name = "%s%d" % (kind, count[kind][0])
+        count[kind][0] += 1
+        inst.then_inc(T.sem[name], 1)
+        made[name] = 1
+        return name
+
+    def need(queue, tag, name, val=None):
+        val = made[name] if val is None else val
+        if (tag, name, val) not in seen:
+            seen.add((tag, name, val))
+            queue.wait_ge(T.sem[name], val)
+
+    def send(dsts, aps, srcs, sem, n, alu=0):
+        mask, k = engines(topo, core, dsts, n)
+        ids = []
+        for d in dsts:
+            a = topo.addr(d)
+            ids.append(DstId(rid=a[0], pnc=a[1]))
+        g.remote_dma_fused([RemoteDMATransfer(dst_ids=ids, dma_engine_mask=mask, remote_sem=T.sem[sem], srcs=srcs,
+                                              dsts=aps, alu_op=alu)], local_sem=T.sem["ls"])
+        nl[0] += k
+
+    def close():
+        used = {s[1] for s in seen}
+        for name in made:
+            if name not in used:
+                g.wait_ge(T.sem[name], made[name])
+        if nl[0]:
+            g.wait_ge(T.sem["ls"], nl[0])
+
+    V, S, P, Y = g.vector, g.scalar, g.tensor, g.sync
+    mx, mn, add = AluOpType.max, AluOpType.min, AluOpType.add
+    NE, NF = 16, 8
+    mk = lambda p, n=MW: T.mk[:, p * MW:p * MW + n]
+    sc = lambda p, a, b: T.sc[:, p * SW + a:p * SW + b]
+    gb = lambda p, a=0, b=L: T.gb[:, p * L + a:p * L + b]
+    pt = lambda p: T.pt[:, p * B:(p + 1) * B]
+    lf = lambda r: T.lf[:, 32 * r:32 * r + 32]
+    en = lambda r: T.en[:, 32 * r:32 * r + 32]
+    pick = lambda r: T.en[:, 32 * r:32 * r + 16]
+    reset = lambda r: T.en[:, 32 * r + 16:32 * r + 32]
+
+    if core in relays[ch]:
+        out = [c for c in mine if relay_of(ch, c) == core]
+        back = [c for c in far if relay_of(ch, c) == core]
+        for c in out:
+            need(g, "g", "mi%d" % rk[c], NE)
+            send(far, [lf(rk[c])] * len(far), [lf(rk[c])], "mi%d" % rk[c], NF)
+        for c in out:
+            need(g, "g", "me%d" % rk[c], NE)
+            send([partner[f] for f in far], [en(rk[c])] * len(far), [en(rk[c])], "me%d" % rk[c], NF)
+        for i, c in enumerate(back):
+            need(g, "g", "rp%d" % rk[c], NE * len(mine))
+            send([c], [T.ld[:, 2 * B:3 * B]], [T.rp[:, (3 * i + k) * B:(3 * i + k + 1) * B] for k in range(3)], "pr2", NF, 2)
+        close()
+        return
+
+    if core in partner.values():
+        o = [c for c in mine if partner[c] == core][0]
+        j = mine.index(o)
+        todo = positions(o, topo, chips, near)[:PS]
+        eneg = ev(V.memset(T.neg[:], -BIG), "v")
+        ez = [ev(V.memset(sc(p, L, SW), 0.0), "v") for p in range(PS)]
+        em = [ev(V.memset(mk(p), BIG), "v") for p in range(PS)]
+        es = []
+        for p, c in enumerate(todo):
+            for e in (eneg, em[p]):
+                need(V, "v", e)
+            need(V, "v", "me%d" % rk[c], NF if c in far else NE)
+            es.append(ev(V.tensor_copy(mk(p).indirect(reset(rk[c])), T.neg[:]), "v"))
+        for p, c in enumerate(todo):
+            need(V, "v", es[p])
+            need(V, "v", "st%d" % p, NE)
+            e = ev(V.tensor_tensor_scan(sc(p, 0, L), mk(p, L), gb(p), -BIG, mn, mx), "v")
+            need(V, "v", ez[p])
+            need(V, "v", e)
+            e = ev(V.tensor_copy(pt(p), sc(p, 0, SW).indirect(pick(rk[c]))), "v")
+            need(g, "g", e)
+            if c in far:
+                rel = relay_of(ch, c)
+                slot = 3 * [f for f in far if relay_of(ch, f) == rel].index(c) + j
+                send([rel], [T.rp[:, slot * B:(slot + 1) * B]], [pt(p)], "rp%d" % rk[c], NE)
+            else:
+                send([c], [T.ld[:, 0:B]], [pt(p)], "pr0", NE)
+        close()
+        return
+    if core not in mine:
+        return
+
+    me = rk[core]
+    j = mine.index(core)
+    todo = positions(core, topo, chips, near)
+    relay = relay_of(ch, core)
+    peers = [c for c in mine if c != core]
+    other = todo[4]
+    scans_mine = [c for c in mine if positions(c, topo, chips, near)[4] == core][0]
+    streams_mine = partner[[c for c in mine if positions(c, topo, chips, near)[0] == core][0]]
+
+    Y.dma_start(T.ix[:], T.idx[:]).then_inc(T.sem["dix"], 16)
+    Y.dma_start(T.tw[:, PAD:PAD + CUT], T.tab[:, 0:CUT]).then_inc(T.sem["dta"], 16)
+    ez2 = ev(V.memset(T.z2[:], 0), "v")
+    S.dma_start(T.x4[:, 0:2], T.end[:]).then_inc(T.sem["den"], 16)
+    S.dma_start(T.x4[8:128, 2:4], T.end[0:15, :]).then_inc(T.sem["den"], 16)
+    S.dma_start(T.z1[0:8, :], T.end[15:16, :]).then_inc(T.sem["den"], 16)
+    need(S, "s", ez2)
+    S.dma_start(T.z2[1:8, :], T.end[15:16, 0:14]).then_inc(T.sem["den"], 16)
+
+    ea = [ev(V.memset(T.sb4[:, 0:2], 1.0 + ZC), "v"), ev(V.memset(T.bs4[:, 0:2], float(ZC)), "v")]
+    eone = ev(V.memset(T.one[:], 1.0), "v")
+    eg = [ev(V.memset(T.tw[:, 0:PAD], -BIG), "v"), ev(V.memset(T.tw[:, PAD + R:W], -BIG), "v")]
+    eneg = ev(V.memset(T.neg[:], -BIG), "v")
+    ez = [ev(V.memset(sc(p, L, SW), 0.0), "v") for p in range(2)]
+    flag = {"allow_small_or_imprecise_dtypes": True}
+    ea.append(ev(g.iota(T.sb4[:, 2:4], [[1, 2]], L, 2, **flag), "q"))
+    ea.append(ev(g.iota(T.bs4[:, 2:4], [[1, 2]], L, 2, **flag), "q"))
+
+    need(V, "v", "dix", 16)
+    eix = ev(V.tensor_copy(lf(me), T.ix[:]), "v")
+    need(g, "g", eix)
+    send(peers + [relay], [lf(me)] * 3, [lf(me)], "mi%d" % me, NE)
+    g.sem_inc(T.sem["pace"], 1)
+    need(Y, "y", "pace", 1)
+    Y.dma_start(T.tw[:, PAD + CUT:PAD + R], T.tab[:, CUT:R]).then_inc(T.sem["dtb"], 16)
+    need(g, "g", eone)
+    eq = ev(g.affine_select(T.qq[:], T.one[:], [[-1, 8], [0, 8], [-8, 16]], AluOpType.is_equal, 0.0, 0, 1), "q")
+
+    need(V, "v", "den", 64)
+    ev0 = ev(V.tensor_copy(T.x4[0:8, 3:4], T.z1[0:8, 0:1]), "v")
+    ev1 = ev(V.tensor_copy(T.x4[0:8, 2:3], T.z2[0:8, 1:2]), "v")
+    for e in ea + [ev0, ev1]:
+        need(V, "v", e)
+    b0 = ev(V.tensor_tensor(T.u4[:], T.x4[:], T.sb4[:], AluOpType.subtract), "v")
+    b1 = ev(V.tensor_tensor(T.ne4[:, 0:2], T.x4[:, 0:2], T.x4[:, 2:4], AluOpType.is_gt), "v")
+    b2 = ev(V.tensor_tensor(T.ne4[:, 2:4], T.x4[:, 0:2], T.x4[:, 2:4], AluOpType.is_gt), "v")
+    for e in (b0, b1, b2):
+        need(V, "v", e)
+    b3 = ev(V.tensor_tensor(T.m4[:], T.u4[:], T.ne4[:], AluOpType.mult), "v")
+    em = [ev(V.memset(mk(0), BIG), "v")]
+    need(V, "v", b3)
+    b4 = ev(V.tensor_tensor(T.r4[:], T.m4[:], T.bs4[:], add), "v")
+    em.append(ev(V.memset(mk(1), BIG), "v"))
+
+    need(P, "p", eq)
+    need(P, "p", b4)
+
+    def mm(out, q, rhs, name):
+        P.matmul(out=out, lhsT=T.qq[:, 128 * q:128 * q + 128], rhs=rhs, start=True, stop=True).then_inc(T.sem[name], 1)
+
+    for h in range(2):
+        for q in range(8):
+            mm(T.pse[:, 16 * h + 2 * q:16 * h + 2 * q + 2], q, T.r4[:, 2 * h:2 * h + 2], "t6")
+    made["t6"] = 16
+    for p, c in enumerate(todo):
+        if c == core:
+            need(P, "p", eix)
+        else:
+            need(P, "p", "mi%d" % rk[c], NF if c in far else NE)
+        for q in range(8):
+            mm(T["ps%d" % p][:, 32 * q:32 * q + 32], q, lf(rk[c]), "t%d" % p)
+        made["t%d" % p] = 8
+
+    need(V, "v", "t6")
+    een = ev(V.tensor_copy(en(me), T.pse[:, 0:32]), "v")
+    need(g, "g", een)
+    send([streams_mine, scans_mine, relay], [en(me)] * 3, [en(me)], "me%d" % me, NE)
+
+    eo = {}
+
+    def convert(p):
+        need(V, "v", "t%d" % p)
+        eo[p] = ev(V.tensor_scalar(T.of[:, 256 * p:256 * p + 256], T["ps%d" % p][:, 0:256], float(PAD - R * me),
+                                   float(PAD + R), add, mn), "v")
+
+    def gather(eng, tag, kind, p, a, b):
+        for e in eg:
+            need(eng, tag, e)
+        need(eng, tag, eo[p])
+        need(eng, tag, "dta", 16)
+        need(eng, tag, "dtb", 16)
+        src = T.tw[:, 0:W].indirect(T.of[:, 256 * p + a // 16:256 * p + b // 16])
+        if tag == "s":
+            return ev(S.activation(gb(p, a, b), src, ActivationFunctionType.Copy), kind)
+        return ev(V.tensor_copy(gb(p, a, b), src), kind)
+
+    def stream(p, evs):
+        for e in evs:
+            need(g, "g", e)
+        send([partner[core]], [gb(p)], [gb(p)], "st%d" % p, NE)
+
+    def scatter(m, r):
+        for e in (eneg, em[m]):
+            need(V, "v", e)
+        return ev(V.tensor_copy(mk(m).indirect(reset(r)), T.neg[:]), "v")
+
+    need(V, "v", een)
+    es1 = scatter(1, me)
+    convert(0)
+    need(V, "v", "me%d" % rk[other], NE)
+    es0 = scatter(0, rk[other])
+
+    cut = [1664, 2048, 2048, 2048, 2048]
+    ends0 = [1984, 3200, L]
+    own = 768
+    hv = gather(V, "v", "v", 0, 0, cut[0])
+    hs = gather(S, "s", "s", 0, cut[0], L)
+    for p in range(1, PS):
+        convert(p)
+    stream(0, [hv, hs])
+    for p in range(1, PS):
+        hv = gather(V, "v", "v", p, 0, cut[p])
+        hs = gather(S, "s", "s", p, cut[p], L)
+        stream(p, [hv, hs])
+        if p == 1:
+            convert(4)
+            convert(5)
+    hv = gather(V, "v", "v", 4, 0, cut[4])
+    hs = gather(S, "s", "s", 4, cut[4], L)
+    ov = gather(V, "v", "v", 5, 0, own)
+    os_ = []
+    a = own
+    for b in ends0:
+        os_.append((a, b, gather(S, "s", "s", 5, a, b)))
+        a = b
+    for e in (es0, es1, hv, hs):
+        need(V, "v", e)
+    e = ev(V.tensor_tensor_scan(sc(0, 0, L), mk(0, L), gb(4), -BIG, mn, mx), "v")
+    for x in ez + [e]:
+        need(V, "v", x)
+    e = ev(V.tensor_copy(pt(0), sc(0, 0, SW).indirect(pick(rk[other]))), "v")
+    need(g, "g", e)
+    send([other], [T.ld[:, B:2 * B]], [pt(0)], "pr1", NE)
+    need(V, "v", ov)
+    e = ev(V.tensor_tensor_scan(sc(1, 0, own), T.mk[:, MW:MW + own], gb(5, 0, own), -BIG, mn, mx), "v")
+    for k, (a, b, h) in enumerate(os_):
+        if k == len(os_) - 1:
+            need(V, "v", "pr0", NE)
+            need(V, "v", "pr2", NF)
+            c0 = ev(V.tensor_tensor(T.cm[:, 0:B], T.ld[:, 0:B], T.ld[:, 2 * B:3 * B], mx), "v")
+        need(V, "v", h)
+        need(V, "v", e)
+        e = ev(V.tensor_tensor_scan(sc(1, a, b), T.mk[:, MW + a:MW + b], gb(5, a, b), sc(1, a - 1, a), mn, mx), "v")
+    need(V, "v", "pr1", NE)
+    need(V, "v", c0)
+    c1 = ev(V.tensor_tensor(T.cm[:, B:2 * B], T.cm[:, 0:B], T.ld[:, B:2 * B], mx), "v")
+    need(V, "v", e)
+    need(V, "v", c1)
+    e = ev(V.tensor_tensor(T.cm[:, 2 * B:3 * B], sc(1, 0, SW).indirect(pick(me)), T.cm[:, B:2 * B], mx), "v")
+    need(Y, "y", e)
+    Y.dma_start(T.y[:], T.cm[:, 2 * B:3 * B]).then_inc(T.sem["dy"], 16)
+    Y.wait_ge(T.sem["dy"], 16)
+    close()

@@ -11,9 +11,14 @@ ZC = L
 SW = L + 8
 MW = L + B
 BIG = 0.999999e30
+HB = 192
 CUT = 10240
 NP = 6
 PS = 4
+VS = [1792, 1792, 1792, 1792, 1856]
+SPLIT = [0, 1, 2, 3]
+A0, AV, AB = 1024, 448, 384
+OWN = [2432, 3392, L]
 
 SCRATCH = {
     "tw": ("sbuf", [128, W], "bfloat16"),
@@ -26,10 +31,11 @@ SCRATCH = {
     "cm": ("sbuf", [128, 3 * B], "bfloat16"),
     "rp": ("sbuf", [128, 9 * B], "bfloat16"),
     "ix": ("sbuf", [128, 32], "int32"),
+    "dg": ("sbuf", [128, 64], "int32"),
     "x4": ("sbuf", [128, 4], "int32"),
     "z1": ("sbuf", [128, 2], "int32"),
     "z2": ("sbuf", [128, 2], "int32"),
-    "lf": ("sbuf", [128, NP * 32], "float32"),
+    "lf": ("sbuf", [128, NP * 64], "bfloat16"),
     "en": ("sbuf", [128, NP * 32], "uint16"),
     "of": ("sbuf", [128, NP * 256], "uint16"),
     "sb4": ("sbuf", [128, 4], "float32"),
@@ -38,16 +44,18 @@ SCRATCH = {
     "ne4": ("sbuf", [128, 4], "float32"),
     "m4": ("sbuf", [128, 4], "float32"),
     "r4": ("sbuf", [128, 4], "float32"),
-    "one": ("sbuf", [128, 1024], "float32"),
-    "qq": ("sbuf", [128, 1024], "float32"),
+    "ci": ("sbuf", [128, 128], "bfloat16"),
+    "pq": ("sbuf", [128, 8], "float32"),
+    "qb": ("sbuf", [128, 2048], "bfloat16"),
+    "qf": ("sbuf", [128, 1024], "float32"),
     "ps0": ("psum", [128, 512], "float32"), "ps1": ("psum", [128, 512], "float32"), "ps2": ("psum", [128, 512], "float32"),
     "ps3": ("psum", [128, 512], "float32"), "ps4": ("psum", [128, 512], "float32"), "ps5": ("psum", [128, 512], "float32"),
     "pse": ("psum", [128, 512], "float32"),
 }
 SEMAPHORES = (["dix", "den", "dta", "dtb", "dy", "pace", "ls", "pr0", "pr1", "pr2"]
               + ["mi%d" % k for k in range(NP)] + ["me%d" % k for k in range(NP)] + ["rp%d" % k for k in range(NP)]
-              + ["st%d" % k for k in range(PS)] + ["v%d" % k for k in range(60)] + ["s%d" % k for k in range(16)]
-              + ["t%d" % k for k in range(8)] + ["q%d" % k for k in range(6)])
+              + ["st%d" % k for k in range(2 * PS)] + ["v%d" % k for k in range(76)] + ["s%d" % k for k in range(18)]
+              + ["t%d" % k for k in range(7)] + ["q%d" % k for k in range(4)])
 
 
 def layout(T, topo):
@@ -71,8 +79,13 @@ def positions(o, topo, chips, near):
     ch = topo.chip(o)
     mine = near[ch]
     j, n = mine.index(o), len(mine)
-    far = [c for k in chips if k != ch for c in near[k]]
-    return [mine[(j + 1) % n]] + far + [mine[(j + 2) % n], o]
+    return [c for k in chips if k != ch for c in near[k]] + [mine[(j + 1) % n], mine[(j + 2) % n], o]
+
+
+def halves(p):
+    if p in SPLIT:
+        return [(0, L // 2, "st%d" % (2 * p)), (L // 2, L, "st%d" % (2 * p + 1))]
+    return [(0, L, "st%d" % (2 * p))]
 
 
 def engines(topo, src, dsts, n):
@@ -93,7 +106,6 @@ def rank_program(g, core, T, topo):
         return
     mine = near[ch]
     far = [c for k in chips if k != ch for c in near[k]]
-    far_chip = [k for k in chips if k != ch][0]
     rk = {c: T.rank_of(c) for c in mine + far}
 
     def relay_of(chip_, c):
@@ -101,7 +113,7 @@ def rank_program(g, core, T, topo):
         return rel[near[topo.chip(c)].index(c) % len(rel)]
 
     made, seen, nl = {}, set(), [0]
-    count = {"v": [0], "s": [0], "t": [0], "q": [0]}
+    count = {"v": [0], "s": [0], "q": [0]}
 
     def ev(inst, kind):
         name = "%s%d" % (kind, count[kind][0])
@@ -110,10 +122,15 @@ def rank_program(g, core, T, topo):
         made[name] = 1
         return name
 
-    def need(queue, tag, name, val=None):
-        val = made[name] if val is None else val
-        if (tag, name, val) not in seen:
-            seen.add((tag, name, val))
+    def need(queue, tag, *names):
+        for name in names:
+            if (tag, name) not in seen:
+                seen.add((tag, name))
+                queue.wait_ge(T.sem[name], made[name])
+
+    def await_(queue, tag, name, val):
+        if (tag, name) not in seen:
+            seen.add((tag, name))
             queue.wait_ge(T.sem[name], val)
 
     def send(dsts, aps, srcs, sem, n, alu=0):
@@ -136,27 +153,33 @@ def rank_program(g, core, T, topo):
 
     V, S, P, Y = g.vector, g.scalar, g.tensor, g.sync
     mx, mn, add = AluOpType.max, AluOpType.min, AluOpType.add
+    COPY = ActivationFunctionType.Copy
     NE, NF = 16, 8
-    mk = lambda p, n=MW: T.mk[:, p * MW:p * MW + n]
+    mk = lambda p, a=0, b=MW: T.mk[:, p * MW + a:p * MW + b]
     sc = lambda p, a, b: T.sc[:, p * SW + a:p * SW + b]
     gb = lambda p, a=0, b=L: T.gb[:, p * L + a:p * L + b]
     pt = lambda p: T.pt[:, p * B:(p + 1) * B]
-    lf = lambda r: T.lf[:, 32 * r:32 * r + 32]
+    lf = lambda r: T.lf[:, 64 * r:64 * r + 64]
     en = lambda r: T.en[:, 32 * r:32 * r + 32]
     pick = lambda r: T.en[:, 32 * r:32 * r + 16]
     reset = lambda r: T.en[:, 32 * r + 16:32 * r + 32]
+
+    def scan(m, p, a, b, last):
+        if a:
+            need(V, "v", last)
+        return ev(V.tensor_tensor_scan(sc(m, a, b), mk(m, a, b), gb(p, a, b), sc(m, a - 1, a) if a else -BIG, mn, mx), "v")
 
     if core in relays[ch]:
         out = [c for c in mine if relay_of(ch, c) == core]
         back = [c for c in far if relay_of(ch, c) == core]
         for c in out:
-            need(g, "g", "mi%d" % rk[c], NE)
+            await_(g, "g", "mi%d" % rk[c], NE)
             send(far, [lf(rk[c])] * len(far), [lf(rk[c])], "mi%d" % rk[c], NF)
         for c in out:
-            need(g, "g", "me%d" % rk[c], NE)
+            await_(g, "g", "me%d" % rk[c], NE)
             send([partner[f] for f in far], [en(rk[c])] * len(far), [en(rk[c])], "me%d" % rk[c], NF)
         for i, c in enumerate(back):
-            need(g, "g", "rp%d" % rk[c], NE * len(mine))
+            await_(g, "g", "rp%d" % rk[c], NE * len(mine))
             send([c], [T.ld[:, 2 * B:3 * B]], [T.rp[:, (3 * i + k) * B:(3 * i + k + 1) * B] for k in range(3)], "pr2", NF, 2)
         close()
         return
@@ -170,17 +193,18 @@ def rank_program(g, core, T, topo):
         em = [ev(V.memset(mk(p), BIG), "v") for p in range(PS)]
         es = []
         for p, c in enumerate(todo):
-            for e in (eneg, em[p]):
-                need(V, "v", e)
-            need(V, "v", "me%d" % rk[c], NF if c in far else NE)
+            need(V, "v", eneg, em[p])
+            await_(V, "v", "me%d" % rk[c], NF if c in far else NE)
             es.append(ev(V.tensor_copy(mk(p).indirect(reset(rk[c])), T.neg[:]), "v"))
         for p, c in enumerate(todo):
             need(V, "v", es[p])
-            need(V, "v", "st%d" % p, NE)
-            e = ev(V.tensor_tensor_scan(sc(p, 0, L), mk(p, L), gb(p), -BIG, mn, mx), "v")
-            need(V, "v", ez[p])
-            need(V, "v", e)
-            e = ev(V.tensor_copy(pt(p), sc(p, 0, SW).indirect(pick(rk[c]))), "v")
+            e = None
+            for a, b, sem in halves(p):
+                await_(V, "v", sem, NE)
+                e = scan(p, p, a, b, e)
+            need(S, "s", ez[p], e)
+            await_(S, "s", "me%d" % rk[c], NF if c in far else NE)
+            e = ev(S.activation(pt(p), sc(p, 0, SW).indirect(pick(rk[c])), COPY), "s")
             need(g, "g", e)
             if c in far:
                 rel = relay_of(ch, c)
@@ -194,164 +218,175 @@ def rank_program(g, core, T, topo):
         return
 
     me = rk[core]
-    j = mine.index(core)
     todo = positions(core, topo, chips, near)
     relay = relay_of(ch, core)
     peers = [c for c in mine if c != core]
-    other = todo[4]
-    scans_mine = [c for c in mine if positions(c, topo, chips, near)[4] == core][0]
-    streams_mine = partner[[c for c in mine if positions(c, topo, chips, near)[0] == core][0]]
+    other = todo[PS]
+    scans_mine = [c for c in mine if positions(c, topo, chips, near)[PS] == core][0]
+    streams_mine = partner[[c for c in mine if positions(c, topo, chips, near)[PS - 1] == core][0]]
 
     Y.dma_start(T.ix[:], T.idx[:]).then_inc(T.sem["dix"], 16)
-    Y.dma_start(T.tw[:, PAD:PAD + CUT], T.tab[:, 0:CUT]).then_inc(T.sem["dta"], 16)
-    ez2 = ev(V.memset(T.z2[:], 0), "v")
     S.dma_start(T.x4[:, 0:2], T.end[:]).then_inc(T.sem["den"], 16)
-    S.dma_start(T.x4[8:128, 2:4], T.end[0:15, :]).then_inc(T.sem["den"], 16)
     S.dma_start(T.z1[0:8, :], T.end[15:16, :]).then_inc(T.sem["den"], 16)
-    need(S, "s", ez2)
-    S.dma_start(T.z2[1:8, :], T.end[15:16, 0:14]).then_inc(T.sem["den"], 16)
+    Y.dma_start(T.x4[8:128, 2:4], T.end[0:15, :]).then_inc(T.sem["den"], 16)
+    Y.dma_start(T.z2[1:8, :], T.end[15:16, 0:14]).then_inc(T.sem["den"], 16)
+    Y.dma_start(T.tw[:, PAD:PAD + CUT], T.tab[:, 0:CUT]).then_inc(T.sem["dta"], 16)
 
-    ea = [ev(V.memset(T.sb4[:, 0:2], 1.0 + ZC), "v"), ev(V.memset(T.bs4[:, 0:2], float(ZC)), "v")]
-    eone = ev(V.memset(T.one[:], 1.0), "v")
-    eg = [ev(V.memset(T.tw[:, 0:PAD], -BIG), "v"), ev(V.memset(T.tw[:, PAD + R:W], -BIG), "v")]
-    eneg = ev(V.memset(T.neg[:], -BIG), "v")
-    ez = [ev(V.memset(sc(p, L, SW), 0.0), "v") for p in range(2)]
     flag = {"allow_small_or_imprecise_dtypes": True}
-    ea.append(ev(g.iota(T.sb4[:, 2:4], [[1, 2]], L, 2, **flag), "q"))
-    ea.append(ev(g.iota(T.bs4[:, 2:4], [[1, 2]], L, 2, **flag), "q"))
+    ei = [ev(g.iota(T.ci[:], [[0, 8], [8, 16]], 0, 0, **flag), "q"), ev(g.iota(T.pq[:], [[-1, 8]], 0, 1, **flag), "q")]
+    ea = [ev(g.iota(T.sb4[:, 2:4], [[1, 2]], L, 2, **flag), "q"), ev(g.iota(T.bs4[:, 2:4], [[1, 2]], L, 2, **flag), "q")]
+    ea.append(ev(V.memset(T.z2[0:1, :], 0), "v"))
+    ea += [ev(V.memset(T.sb4[:, 0:2], 1.0 + ZC), "v"), ev(V.memset(T.bs4[:, 0:2], float(ZC)), "v")]
+    eg = [ev(V.memset(T.tw[:, 0:PAD], -BIG), "v"), ev(V.memset(T.tw[:, PAD + R:W], -BIG), "v")]
+    need(V, "v", *ei)
+    qb = lambda q: T.qb[:, 128 * q:128 * q + 128]
+    eq = [ev(V.tensor_scalar(qb(q), T.ci[:], T.pq[:, q:q + 1], None, AluOpType.is_equal), "v") for q in range(8)]
+    need(S, "s", *eq)
+    eqf = ev(S.activation(T.qf[:], T.qb[:, 0:1024], COPY), "s")
 
-    need(V, "v", "dix", 16)
-    eix = ev(V.tensor_copy(lf(me), T.ix[:]), "v")
-    need(g, "g", eix)
+    await_(V, "v", "dix", 16)
+    d0 = ev(V.tensor_scalar(T.dg[:, 0:32], T.ix[:], 8, None, AluOpType.arith_shift_right), "v")
+    d1 = ev(V.tensor_scalar(T.dg[:, 32:64], T.ix[:], 255, None, AluOpType.bitwise_and), "v")
+    need(V, "v", d0)
+    x = 64 * me
+    eix = [ev(V.tensor_scalar(T.lf[:, x:x + 32], T.dg[:, 0:32], float(-HB), None, add), "v")]
+    need(V, "v", d1)
+    eix.append(ev(V.tensor_copy(T.lf[:, x + 32:x + 64], T.dg[:, 32:64]), "v"))
+    need(g, "g", *eix)
     send(peers + [relay], [lf(me)] * 3, [lf(me)], "mi%d" % me, NE)
     g.sem_inc(T.sem["pace"], 1)
-    need(Y, "y", "pace", 1)
+    await_(Y, "y", "pace", 1)
     Y.dma_start(T.tw[:, PAD + CUT:PAD + R], T.tab[:, CUT:R]).then_inc(T.sem["dtb"], 16)
-    need(g, "g", eone)
-    eq = ev(g.affine_select(T.qq[:], T.one[:], [[-1, 8], [0, 8], [-8, 16]], AluOpType.is_equal, 0.0, 0, 1), "q")
+    eq += [ev(V.tensor_scalar(qb(8 + q), T.ci[:], T.pq[:, q:q + 1], 256.0, AluOpType.is_equal, AluOpType.mult), "v")
+           for q in range(8)]
 
-    need(V, "v", "den", 64)
-    ev0 = ev(V.tensor_copy(T.x4[0:8, 3:4], T.z1[0:8, 0:1]), "v")
-    ev1 = ev(V.tensor_copy(T.x4[0:8, 2:3], T.z2[0:8, 1:2]), "v")
-    for e in ea + [ev0, ev1]:
-        need(V, "v", e)
+    await_(V, "v", "den", 64)
+    x0 = ev(V.tensor_copy(T.x4[0:8, 3:4], T.z1[0:8, 0:1]), "v")
+    x1 = ev(V.tensor_copy(T.x4[0:8, 2:3], T.z2[0:8, 1:2]), "v")
+    need(V, "v", x0, x1, *ea)
     b0 = ev(V.tensor_tensor(T.u4[:], T.x4[:], T.sb4[:], AluOpType.subtract), "v")
     b1 = ev(V.tensor_tensor(T.ne4[:, 0:2], T.x4[:, 0:2], T.x4[:, 2:4], AluOpType.is_gt), "v")
     b2 = ev(V.tensor_tensor(T.ne4[:, 2:4], T.x4[:, 0:2], T.x4[:, 2:4], AluOpType.is_gt), "v")
-    for e in (b0, b1, b2):
-        need(V, "v", e)
+    eneg = ev(V.memset(T.neg[:], -BIG), "v")
+    need(V, "v", b0, b1, b2)
     b3 = ev(V.tensor_tensor(T.m4[:], T.u4[:], T.ne4[:], AluOpType.mult), "v")
-    em = [ev(V.memset(mk(0), BIG), "v")]
+    ez = [ev(V.memset(sc(p, L, SW), 0.0), "v") for p in range(2)]
     need(V, "v", b3)
     b4 = ev(V.tensor_tensor(T.r4[:], T.m4[:], T.bs4[:], add), "v")
-    em.append(ev(V.memset(mk(1), BIG), "v"))
+    em = [[ev(V.memset(mk(0), BIG), "v")]]
+    need(S, "s", *eq)
+    em.append([ev(S.activation(mk(1, a, a + 2048), T.qb[:], ActivationFunctionType.Identity, bias=BIG, scale=0.0), "s")
+               for a in (0, L // 2)])
 
-    need(P, "p", eq)
-    need(P, "p", b4)
+    def mm(out, lhs, rhs, name, start=True, stop=True):
+        P.matmul(out=out, lhsT=lhs, rhs=rhs, start=start, stop=stop).then_inc(T.sem[name], 1)
 
-    def mm(out, q, rhs, name):
-        P.matmul(out=out, lhsT=T.qq[:, 128 * q:128 * q + 128], rhs=rhs, start=True, stop=True).then_inc(T.sem[name], 1)
-
-    for h in range(2):
-        for q in range(8):
-            mm(T.pse[:, 16 * h + 2 * q:16 * h + 2 * q + 2], q, T.r4[:, 2 * h:2 * h + 2], "t6")
-    made["t6"] = 16
-    for p, c in enumerate(todo):
+    need(P, "p", *eq)
+    for p in [5, None, 3, 4, 0, 1, 2]:
+        if p is None:
+            need(P, "p", eqf, b4)
+            for q in range(8):
+                mm(T.pse[:, 4 * q:4 * q + 4], T.qf[:, 128 * q:128 * q + 128], T.r4[:], "t6")
+            made["t6"] = 8
+            continue
+        c = todo[p]
         if c == core:
-            need(P, "p", eix)
+            need(P, "p", *eix)
         else:
-            need(P, "p", "mi%d" % rk[c], NF if c in far else NE)
+            await_(P, "p", "mi%d" % rk[c], NF if c in far else NE)
+        x = 64 * rk[c]
         for q in range(8):
-            mm(T["ps%d" % p][:, 32 * q:32 * q + 32], q, lf(rk[c]), "t%d" % p)
-        made["t%d" % p] = 8
-
-    need(V, "v", "t6")
-    een = ev(V.tensor_copy(en(me), T.pse[:, 0:32]), "v")
-    need(g, "g", een)
-    send([streams_mine, scans_mine, relay], [en(me)] * 3, [en(me)], "me%d" % me, NE)
+            o = T["ps%d" % p][:, 32 * q:32 * q + 32]
+            mm(o, qb(8 + q), T.lf[:, x:x + 32], "t%d" % p, True, False)
+            mm(o, qb(q), T.lf[:, x + 32:x + 64], "t%d" % p, False, True)
+        made["t%d" % p] = 16
 
     eo = {}
 
     def convert(p):
         need(V, "v", "t%d" % p)
-        eo[p] = ev(V.tensor_scalar(T.of[:, 256 * p:256 * p + 256], T["ps%d" % p][:, 0:256], float(PAD - R * me),
-                                   float(PAD + R), add, mn), "v")
+        eo[p] = ev(V.tensor_scalar(T.of[:, 256 * p:256 * p + 256], T["ps%d" % p][:, 0:256],
+                                   float(256 * HB + PAD - R * me), float(PAD + R), add, mn), "v")
 
-    def gather(eng, tag, kind, p, a, b):
-        for e in eg:
-            need(eng, tag, e)
-        need(eng, tag, eo[p])
-        need(eng, tag, "dta", 16)
-        need(eng, tag, "dtb", 16)
+    def gather(tag, p, a, b):
+        eng = V if tag == "v" else S
+        need(eng, tag, eo[p], *eg)
+        await_(eng, tag, "dta", 16)
+        await_(eng, tag, "dtb", 16)
         src = T.tw[:, 0:W].indirect(T.of[:, 256 * p + a // 16:256 * p + b // 16])
         if tag == "s":
-            return ev(S.activation(gb(p, a, b), src, ActivationFunctionType.Copy), kind)
-        return ev(V.tensor_copy(gb(p, a, b), src), kind)
-
-    def stream(p, evs):
-        for e in evs:
-            need(g, "g", e)
-        send([partner[core]], [gb(p)], [gb(p)], "st%d" % p, NE)
+            return ev(S.activation(gb(p, a, b), src, COPY), tag)
+        return ev(V.tensor_copy(gb(p, a, b), src), tag)
 
     def scatter(m, r):
-        for e in (eneg, em[m]):
-            need(V, "v", e)
+        need(V, "v", eneg, *em[m])
         return ev(V.tensor_copy(mk(m).indirect(reset(r)), T.neg[:]), "v")
 
-    need(V, "v", een)
+    convert(5)
+    need(V, "v", "t6")
+    een = []
+    for h in range(2):
+        for k in range(2):
+            x = 32 * me + 16 * h + k
+            een.append(ev(V.tensor_copy(T.en[:, x:x + 15:2], T.pse[:, 2 * h + k:32:4]), "v"))
+    need(g, "g", *een)
+    send([streams_mine, scans_mine, relay], [en(me)] * 3, [en(me)], "me%d" % me, NE)
+    need(V, "v", *een)
     es1 = scatter(1, me)
-    convert(0)
-    need(V, "v", "me%d" % rk[other], NE)
-    es0 = scatter(0, rk[other])
+    convert(3)
+    convert(4)
 
-    cut = [1664, 2048, 2048, 2048, 2048]
-    ends0 = [1984, 3200, L]
-    own = 768
-    hv = gather(V, "v", "v", 0, 0, cut[0])
-    hs = gather(S, "s", "s", 0, cut[0], L)
-    for p in range(1, PS):
-        convert(p)
-    stream(0, [hv, hs])
-    for p in range(1, PS):
-        hv = gather(V, "v", "v", p, 0, cut[p])
-        hs = gather(S, "s", "s", p, cut[p], L)
-        stream(p, [hv, hs])
-        if p == 1:
-            convert(4)
-            convert(5)
-    hv = gather(V, "v", "v", 4, 0, cut[4])
-    hs = gather(S, "s", "s", 4, cut[4], L)
-    ov = gather(V, "v", "v", 5, 0, own)
-    os_ = []
-    a = own
-    for b in ends0:
-        os_.append((a, b, gather(S, "s", "s", 5, a, b)))
+    ov = gather("v", 5, 0, AV)
+    osa = gather("s", 5, AV, A0)
+    convert(0)
+    for p in range(PS):
+        cut = halves(p)
+        for a, b, sem in cut:
+            m = a + VS[p] // len(cut)
+            hv = gather("v", p, a, m)
+            hs = gather("s", p, m, b)
+            need(g, "g", hv, hs)
+            send([partner[core]], [gb(p, a, b)], [gb(p, a, b)], sem, NE)
+        if p == 0:
+            convert(1)
+            convert(2)
+        if p == 2:
+            await_(V, "v", "me%d" % rk[other], NE)
+            es0 = scatter(0, rk[other])
+    nv = gather("v", 4, 0, VS[4])
+    ns = gather("s", 4, VS[4], L)
+    parts = []
+    a = A0
+    if AB:
+        parts.append((a, a + AB, gather("v", 5, a, a + AB)))
+        a += AB
+    for b in OWN:
+        parts.append((a, b, gather("s", 5, a, b)))
         a = b
-    for e in (es0, es1, hv, hs):
-        need(V, "v", e)
-    e = ev(V.tensor_tensor_scan(sc(0, 0, L), mk(0, L), gb(4), -BIG, mn, mx), "v")
-    for x in ez + [e]:
-        need(V, "v", x)
-    e = ev(V.tensor_copy(pt(0), sc(0, 0, SW).indirect(pick(rk[other]))), "v")
-    need(g, "g", e)
+
+    need(V, "v", es0, nv)
+    e0 = scan(0, 4, 0, VS[4], None)
+    need(V, "v", es1, ov, osa)
+    e1 = scan(1, 5, 0, A0, None)
+    need(V, "v", ns)
+    e0 = scan(0, 4, VS[4], L, e0)
+    need(V, "v", e0, *ez)
+    e0 = ev(V.tensor_copy(pt(0), sc(0, 0, SW).indirect(pick(rk[other]))), "v")
+    need(g, "g", e0)
     send([other], [T.ld[:, B:2 * B]], [pt(0)], "pr1", NE)
-    need(V, "v", ov)
-    e = ev(V.tensor_tensor_scan(sc(1, 0, own), T.mk[:, MW:MW + own], gb(5, 0, own), -BIG, mn, mx), "v")
-    for k, (a, b, h) in enumerate(os_):
-        if k == len(os_) - 1:
-            need(V, "v", "pr0", NE)
-            need(V, "v", "pr2", NF)
+    for k, (a, b, h) in enumerate(parts):
+        if k == len(parts) - 1:
+            await_(V, "v", "pr0", NE)
+            await_(V, "v", "pr2", NF)
             c0 = ev(V.tensor_tensor(T.cm[:, 0:B], T.ld[:, 0:B], T.ld[:, 2 * B:3 * B], mx), "v")
+            await_(V, "v", "pr1", NE)
+            need(V, "v", c0)
+            c1 = ev(V.tensor_tensor(T.cm[:, B:2 * B], T.cm[:, 0:B], T.ld[:, B:2 * B], mx), "v")
         need(V, "v", h)
-        need(V, "v", e)
-        e = ev(V.tensor_tensor_scan(sc(1, a, b), T.mk[:, MW + a:MW + b], gb(5, a, b), sc(1, a - 1, a), mn, mx), "v")
-    need(V, "v", "pr1", NE)
-    need(V, "v", c0)
-    c1 = ev(V.tensor_tensor(T.cm[:, B:2 * B], T.cm[:, 0:B], T.ld[:, B:2 * B], mx), "v")
-    need(V, "v", e)
-    need(V, "v", c1)
-    e = ev(V.tensor_tensor(T.cm[:, 2 * B:3 * B], sc(1, 0, SW).indirect(pick(me)), T.cm[:, B:2 * B], mx), "v")
-    need(Y, "y", e)
+        e1 = scan(1, 5, a, b, e1)
+    need(V, "v", e1, c1)
+    e1 = ev(V.tensor_tensor(T.cm[:, 2 * B:3 * B], sc(1, 0, SW).indirect(pick(me)), T.cm[:, B:2 * B], mx), "v")
+    need(Y, "y", e1)
     Y.dma_start(T.y[:], T.cm[:, 2 * B:3 * B]).then_inc(T.sem["dy"], 16)
     Y.wait_ge(T.sem["dy"], 16)
     close()

from concourse.bass import DstId, RemoteDMATransfer
from concourse.mybir import AluOpType, ActivationFunctionType

SIM = 16
R = 16384
L = 4096
B = 256
PAD = 8
W = R + 2 * PAD
ZC = L
SW = L + 8
MW = L + B
BIG = 0.999999e30
HB = 192
CUT = 10240
NP = 6
PS = 4
VS = [1792, 1792, 1792, 1792, 1856]
SPLIT = [0, 1, 2, 3]
A0, AV, AB = 1024, 448, 384
OWN = [2432, 3392, L]

SCRATCH = {
    "tw": ("sbuf", [128, W], "bfloat16"),
    "gb": ("sbuf", [128, NP * L], "bfloat16"),
    "mk": ("sbuf", [128, PS * MW], "bfloat16"),
    "sc": ("sbuf", [128, PS * SW], "bfloat16"),
    "neg": ("sbuf", [128, B], "bfloat16"),
    "pt": ("sbuf", [128, PS * B], "bfloat16"),
    "ld": ("sbuf", [128, 3 * B], "bfloat16"),
    "cm": ("sbuf", [128, 3 * B], "bfloat16"),
    "rp": ("sbuf", [128, 9 * B], "bfloat16"),
    "ix": ("sbuf", [128, 32], "int32"),
    "dg": ("sbuf", [128, 64], "int32"),
    "x4": ("sbuf", [128, 4], "int32"),
    "z1": ("sbuf", [128, 2], "int32"),
    "z2": ("sbuf", [128, 2], "int32"),
    "lf": ("sbuf", [128, NP * 64], "bfloat16"),
    "en": ("sbuf", [128, NP * 32], "uint16"),
    "of": ("sbuf", [128, NP * 256], "uint16"),
    "sb4": ("sbuf", [128, 4], "float32"),
    "bs4": ("sbuf", [128, 4], "float32"),
    "u4": ("sbuf", [128, 4], "float32"),
    "ne4": ("sbuf", [128, 4], "float32"),
    "m4": ("sbuf", [128, 4], "float32"),
    "r4": ("sbuf", [128, 4], "float32"),
    "ci": ("sbuf", [128, 128], "bfloat16"),
    "pq": ("sbuf", [128, 8], "float32"),
    "qb": ("sbuf", [128, 2048], "bfloat16"),
    "qf": ("sbuf", [128, 1024], "float32"),
    "ps0": ("psum", [128, 512], "float32"), "ps1": ("psum", [128, 512], "float32"), "ps2": ("psum", [128, 512], "float32"),
    "ps3": ("psum", [128, 512], "float32"), "ps4": ("psum", [128, 512], "float32"), "ps5": ("psum", [128, 512], "float32"),
    "pse": ("psum", [128, 512], "float32"),
}
SEMAPHORES = (["dix", "den", "dta", "dtb", "dy", "pace", "ls", "pr0", "pr1", "pr2"]
              + ["mi%d" % k for k in range(NP)] + ["me%d" % k for k in range(NP)] + ["rp%d" % k for k in range(NP)]
              + ["st%d" % k for k in range(2 * PS)] + ["v%d" % k for k in range(76)] + ["s%d" % k for k in range(18)]
              + ["t%d" % k for k in range(7)] + ["q%d" % k for k in range(4)])


def layout(T, topo):
    ranks = list(T.cores)
    chips = sorted({topo.chip(c) for c in ranks})
    near, relays, partner = {}, {}, {}
    for ch in chips:
        here = [c for c in range(SIM) if topo.chip(c) == ch]
        away = [c for c in range(SIM) if topo.chip(c) in chips and topo.chip(c) != ch]
        near[ch] = [c for c in here if c in ranks]
        spare = [c for c in here if c not in ranks]
        port = {c: all(topo.may_write(c, d) for d in away) for c in spare}
        for o in near[ch]:
            free = [c for c in spare if c not in partner.values()]
            partner[o] = min(free, key=lambda c: (topo.die(c) != topo.die(o), port[c], c))
        relays[ch] = [c for c in spare if port[c] and c not in partner.values()]
    return chips, near, relays, partner


def positions(o, topo, chips, near):
    ch = topo.chip(o)
    mine = near[ch]
    j, n = mine.index(o), len(mine)
    return [c for k in chips if k != ch for c in near[k]] + [mine[(j + 1) % n], mine[(j + 2) % n], o]


def halves(p):
    if p in SPLIT:
        return [(0, L // 2, "st%d" % (2 * p)), (L // 2, L, "st%d" % (2 * p + 1))]
    return [(0, L, "st%d" % (2 * p))]


def engines(topo, src, dsts, n):
    m = None
    for d in dsts:
        m = topo.mask(src, d) if m is None else m & topo.mask(src, d)
    out, k = 0, 0
    for b in range(m.bit_length()):
        if (m >> b) & 1 and k < n:
            out, k = out | (1 << b), k + 1
    return out, k


def rank_program(g, core, T, topo):
    chips, near, relays, partner = layout(T, topo)
    ch = topo.chip(core)
    if ch not in chips:
        return
    mine = near[ch]
    far = [c for k in chips if k != ch for c in near[k]]
    rk = {c: T.rank_of(c) for c in mine + far}

    def relay_of(chip_, c):
        rel = relays[chip_]
        return rel[near[topo.chip(c)].index(c) % len(rel)]

    made, seen, nl = {}, set(), [0]
    count = {"v": [0], "s": [0], "q": [0]}

    def ev(inst, kind):
        name = "%s%d" % (kind, count[kind][0])
        count[kind][0] += 1
        inst.then_inc(T.sem[name], 1)
        made[name] = 1
        return name

    def need(queue, tag, *names):
        for name in names:
            if (tag, name) not in seen:
                seen.add((tag, name))
                queue.wait_ge(T.sem[name], made[name])

    def await_(queue, tag, name, val):
        if (tag, name) not in seen:
            seen.add((tag, name))
            queue.wait_ge(T.sem[name], val)

    def send(dsts, aps, srcs, sem, n, alu=0):
        mask, k = engines(topo, core, dsts, n)
        ids = []
        for d in dsts:
            a = topo.addr(d)
            ids.append(DstId(rid=a[0], pnc=a[1]))
        g.remote_dma_fused([RemoteDMATransfer(dst_ids=ids, dma_engine_mask=mask, remote_sem=T.sem[sem], srcs=srcs,
                                              dsts=aps, alu_op=alu)], local_sem=T.sem["ls"])
        nl[0] += k

    def close():
        used = {s[1] for s in seen}
        for name in made:
            if name not in used:
                g.wait_ge(T.sem[name], made[name])
        if nl[0]:
            g.wait_ge(T.sem["ls"], nl[0])

    V, S, P, Y = g.vector, g.scalar, g.tensor, g.sync
    mx, mn, add = AluOpType.max, AluOpType.min, AluOpType.add
    COPY = ActivationFunctionType.Copy
    NE, NF = 16, 8
    mk = lambda p, a=0, b=MW: T.mk[:, p * MW + a:p * MW + b]
    sc = lambda p, a, b: T.sc[:, p * SW + a:p * SW + b]
    gb = lambda p, a=0, b=L: T.gb[:, p * L + a:p * L + b]
    pt = lambda p: T.pt[:, p * B:(p + 1) * B]
    lf = lambda r: T.lf[:, 64 * r:64 * r + 64]
    en = lambda r: T.en[:, 32 * r:32 * r + 32]
    pick = lambda r: T.en[:, 32 * r:32 * r + 16]
    reset = lambda r: T.en[:, 32 * r + 16:32 * r + 32]

    def scan(m, p, a, b, last):
        if a:
            need(V, "v", last)
        return ev(V.tensor_tensor_scan(sc(m, a, b), mk(m, a, b), gb(p, a, b), sc(m, a - 1, a) if a else -BIG, mn, mx), "v")

    if core in relays[ch]:
        out = [c for c in mine if relay_of(ch, c) == core]
        back = [c for c in far if relay_of(ch, c) == core]
        for c in out:
            await_(g, "g", "mi%d" % rk[c], NE)
            send(far, [lf(rk[c])] * len(far), [lf(rk[c])], "mi%d" % rk[c], NF)
        for c in out:
            await_(g, "g", "me%d" % rk[c], NE)
            send([partner[f] for f in far], [en(rk[c])] * len(far), [en(rk[c])], "me%d" % rk[c], NF)
        for i, c in enumerate(back):
            await_(g, "g", "rp%d" % rk[c], NE * len(mine))
            send([c], [T.ld[:, 2 * B:3 * B]], [T.rp[:, (3 * i + k) * B:(3 * i + k + 1) * B] for k in range(3)], "pr2", NF, 2)
        close()
        return

    if core in partner.values():
        o = [c for c in mine if partner[c] == core][0]
        j = mine.index(o)
        todo = positions(o, topo, chips, near)[:PS]
        eneg = ev(V.memset(T.neg[:], -BIG), "v")
        ez = [ev(V.memset(sc(p, L, SW), 0.0), "v") for p in range(PS)]
        em = [ev(V.memset(mk(p), BIG), "v") for p in range(PS)]
        es = []
        for p, c in enumerate(todo):
            need(V, "v", eneg, em[p])
            await_(V, "v", "me%d" % rk[c], NF if c in far else NE)
            es.append(ev(V.tensor_copy(mk(p).indirect(reset(rk[c])), T.neg[:]), "v"))
        for p, c in enumerate(todo):
            need(V, "v", es[p])
            e = None
            for a, b, sem in halves(p):
                await_(V, "v", sem, NE)
                e = scan(p, p, a, b, e)
            need(S, "s", ez[p], e)
            await_(S, "s", "me%d" % rk[c], NF if c in far else NE)
            e = ev(S.activation(pt(p), sc(p, 0, SW).indirect(pick(rk[c])), COPY), "s")
            need(g, "g", e)
            if c in far:
                rel = relay_of(ch, c)
                slot = 3 * [f for f in far if relay_of(ch, f) == rel].index(c) + j
                send([rel], [T.rp[:, slot * B:(slot + 1) * B]], [pt(p)], "rp%d" % rk[c], NE)
            else:
                send([c], [T.ld[:, 0:B]], [pt(p)], "pr0", NE)
        close()
        return
    if core not in mine:
        return

    me = rk[core]
    todo = positions(core, topo, chips, near)
    relay = relay_of(ch, core)
    peers = [c for c in mine if c != core]
    other = todo[PS]
    scans_mine = [c for c in mine if positions(c, topo, chips, near)[PS] == core][0]
    streams_mine = partner[[c for c in mine if positions(c, topo, chips, near)[PS - 1] == core][0]]

    Y.dma_start(T.ix[:], T.idx[:]).then_inc(T.sem["dix"], 16)
    S.dma_start(T.x4[:, 0:2], T.end[:]).then_inc(T.sem["den"], 16)
    S.dma_start(T.z1[0:8, :], T.end[15:16, :]).then_inc(T.sem["den"], 16)
    Y.dma_start(T.x4[8:128, 2:4], T.end[0:15, :]).then_inc(T.sem["den"], 16)
    Y.dma_start(T.z2[1:8, :], T.end[15:16, 0:14]).then_inc(T.sem["den"], 16)
    Y.dma_start(T.tw[:, PAD:PAD + CUT], T.tab[:, 0:CUT]).then_inc(T.sem["dta"], 16)

    flag = {"allow_small_or_imprecise_dtypes": True}
    ei = [ev(g.iota(T.ci[:], [[0, 8], [8, 16]], 0, 0, **flag), "q"), ev(g.iota(T.pq[:], [[-1, 8]], 0, 1, **flag), "q")]
    ea = [ev(g.iota(T.sb4[:, 2:4], [[1, 2]], L, 2, **flag), "q"), ev(g.iota(T.bs4[:, 2:4], [[1, 2]], L, 2, **flag), "q")]
    ea.append(ev(V.memset(T.z2[0:1, :], 0), "v"))
    ea += [ev(V.memset(T.sb4[:, 0:2], 1.0 + ZC), "v"), ev(V.memset(T.bs4[:, 0:2], float(ZC)), "v")]
    eg = [ev(V.memset(T.tw[:, 0:PAD], -BIG), "v"), ev(V.memset(T.tw[:, PAD + R:W], -BIG), "v")]
    need(V, "v", *ei)
    qb = lambda q: T.qb[:, 128 * q:128 * q + 128]
    eq = [ev(V.tensor_scalar(qb(q), T.ci[:], T.pq[:, q:q + 1], None, AluOpType.is_equal), "v") for q in range(8)]
    need(S, "s", *eq)
    eqf = ev(S.activation(T.qf[:], T.qb[:, 0:1024], COPY), "s")

    await_(V, "v", "dix", 16)
    d0 = ev(V.tensor_scalar(T.dg[:, 0:32], T.ix[:], 8, None, AluOpType.arith_shift_right), "v")
    d1 = ev(V.tensor_scalar(T.dg[:, 32:64], T.ix[:], 255, None, AluOpType.bitwise_and), "v")
    need(V, "v", d0)
    x = 64 * me
    eix = [ev(V.tensor_scalar(T.lf[:, x:x + 32], T.dg[:, 0:32], float(-HB), None, add), "v")]
    need(V, "v", d1)
    eix.append(ev(V.tensor_copy(T.lf[:, x + 32:x + 64], T.dg[:, 32:64]), "v"))
    need(g, "g", *eix)
    send(peers + [relay], [lf(me)] * 3, [lf(me)], "mi%d" % me, NE)
    g.sem_inc(T.sem["pace"], 1)
    await_(Y, "y", "pace", 1)
    Y.dma_start(T.tw[:, PAD + CUT:PAD + R], T.tab[:, CUT:R]).then_inc(T.sem["dtb"], 16)
    eq += [ev(V.tensor_scalar(qb(8 + q), T.ci[:], T.pq[:, q:q + 1], 256.0, AluOpType.is_equal, AluOpType.mult), "v")
           for q in range(8)]

    await_(V, "v", "den", 64)
    x0 = ev(V.tensor_copy(T.x4[0:8, 3:4], T.z1[0:8, 0:1]), "v")
    x1 = ev(V.tensor_copy(T.x4[0:8, 2:3], T.z2[0:8, 1:2]), "v")
    need(V, "v", x0, x1, *ea)
    b0 = ev(V.tensor_tensor(T.u4[:], T.x4[:], T.sb4[:], AluOpType.subtract), "v")
    b1 = ev(V.tensor_tensor(T.ne4[:, 0:2], T.x4[:, 0:2], T.x4[:, 2:4], AluOpType.is_gt), "v")
    b2 = ev(V.tensor_tensor(T.ne4[:, 2:4], T.x4[:, 0:2], T.x4[:, 2:4], AluOpType.is_gt), "v")
    eneg = ev(V.memset(T.neg[:], -BIG), "v")
    need(V, "v", b0, b1, b2)
    b3 = ev(V.tensor_tensor(T.m4[:], T.u4[:], T.ne4[:], AluOpType.mult), "v")
    ez = [ev(V.memset(sc(p, L, SW), 0.0), "v") for p in range(2)]
    need(V, "v", b3)
    b4 = ev(V.tensor_tensor(T.r4[:], T.m4[:], T.bs4[:], add), "v")
    em = [[ev(V.memset(mk(0), BIG), "v")]]
    need(S, "s", *eq)
    em.append([ev(S.activation(mk(1, a, a + 2048), T.qb[:], ActivationFunctionType.Identity, bias=BIG, scale=0.0), "s")
               for a in (0, L // 2)])

    def mm(out, lhs, rhs, name, start=True, stop=True):
        P.matmul(out=out, lhsT=lhs, rhs=rhs, start=start, stop=stop).then_inc(T.sem[name], 1)

    need(P, "p", *eq)
    for p in [5, None, 3, 4, 0, 1, 2]:
        if p is None:
            need(P, "p", eqf, b4)
            for q in range(8):
                mm(T.pse[:, 4 * q:4 * q + 4], T.qf[:, 128 * q:128 * q + 128], T.r4[:], "t6")
            made["t6"] = 8
            continue
        c = todo[p]
        if c == core:
            need(P, "p", *eix)
        else:
            await_(P, "p", "mi%d" % rk[c], NF if c in far else NE)
        x = 64 * rk[c]
        for q in range(8):
            o = T["ps%d" % p][:, 32 * q:32 * q + 32]
            mm(o, qb(8 + q), T.lf[:, x:x + 32], "t%d" % p, True, False)
            mm(o, qb(q), T.lf[:, x + 32:x + 64], "t%d" % p, False, True)
        made["t%d" % p] = 16

    eo = {}

    def convert(p):
        need(V, "v", "t%d" % p)
        eo[p] = ev(V.tensor_scalar(T.of[:, 256 * p:256 * p + 256], T["ps%d" % p][:, 0:256],
                                   float(256 * HB + PAD - R * me), float(PAD + R), add, mn), "v")

    def gather(tag, p, a, b):
        eng = V if tag == "v" else S
        need(eng, tag, eo[p], *eg)
        await_(eng, tag, "dta", 16)
        await_(eng, tag, "dtb", 16)
        src = T.tw[:, 0:W].indirect(T.of[:, 256 * p + a // 16:256 * p + b // 16])
        if tag == "s":
            return ev(S.activation(gb(p, a, b), src, COPY), tag)
        return ev(V.tensor_copy(gb(p, a, b), src), tag)

    def scatter(m, r):
        need(V, "v", eneg, *em[m])
        return ev(V.tensor_copy(mk(m).indirect(reset(r)), T.neg[:]), "v")

    convert(5)
    need(V, "v", "t6")
    een = []
    for h in range(2):
        for k in range(2):
            x = 32 * me + 16 * h + k
            een.append(ev(V.tensor_copy(T.en[:, x:x + 15:2], T.pse[:, 2 * h + k:32:4]), "v"))
    need(g, "g", *een)
    send([streams_mine, scans_mine, relay], [en(me)] * 3, [en(me)], "me%d" % me, NE)
    need(V, "v", *een)
    es1 = scatter(1, me)
    convert(3)
    convert(4)

    ov = gather("v", 5, 0, AV)
    osa = gather("s", 5, AV, A0)
    convert(0)
    for p in range(PS):
        cut = halves(p)
        for a, b, sem in cut:
            m = a + VS[p] // len(cut)
            hv = gather("v", p, a, m)
            hs = gather("s", p, m, b)
            need(g, "g", hv, hs)
            send([partner[core]], [gb(p, a, b)], [gb(p, a, b)], sem, NE)
        if p == 0:
            convert(1)
            convert(2)
        if p == 2:
            await_(V, "v", "me%d" % rk[other], NE)
            es0 = scatter(0, rk[other])
    nv = gather("v", 4, 0, VS[4])
    ns = gather("s", 4, VS[4], L)
    parts = []
    a = A0
    if AB:
        parts.append((a, a + AB, gather("v", 5, a, a + AB)))
        a += AB
    for b in OWN:
        parts.append((a, b, gather("s", 5, a, b)))
        a = b

    need(V, "v", es0, nv)
    e0 = scan(0, 4, 0, VS[4], None)
    need(V, "v", es1, ov, osa)
    e1 = scan(1, 5, 0, A0, None)
    need(V, "v", ns)
    e0 = scan(0, 4, VS[4], L, e0)
    need(V, "v", e0, *ez)
    e0 = ev(V.tensor_copy(pt(0), sc(0, 0, SW).indirect(pick(rk[other]))), "v")
    need(g, "g", e0)
    send([other], [T.ld[:, B:2 * B]], [pt(0)], "pr1", NE)
    for k, (a, b, h) in enumerate(parts):
        if k == len(parts) - 1:
            await_(V, "v", "pr0", NE)
            await_(V, "v", "pr2", NF)
            c0 = ev(V.tensor_tensor(T.cm[:, 0:B], T.ld[:, 0:B], T.ld[:, 2 * B:3 * B], mx), "v")
            await_(V, "v", "pr1", NE)
            need(V, "v", c0)
            c1 = ev(V.tensor_tensor(T.cm[:, B:2 * B], T.cm[:, 0:B], T.ld[:, B:2 * B], mx), "v")
        need(V, "v", h)
        e1 = scan(1, 5, a, b, e1)
    need(V, "v", e1, c1)
    e1 = ev(V.tensor_tensor(T.cm[:, 2 * B:3 * B], sc(1, 0, SW).indirect(pick(me)), T.cm[:, B:2 * B], mx), "v")
    need(Y, "y", e1)
    Y.dma_start(T.y[:], T.cm[:, 2 * B:3 * B]).then_inc(T.sem["dy"], 16)
    Y.wait_ge(T.sem["dy"], 16)
    close()
